import numpy as np
import ml_dtypes


def mxq(x, axis, fmt="e4m3"):
    dtype, down = {"e4m3": (ml_dtypes.float8_e4m3fn, 7), "e5m2": (ml_dtypes.float8_e5m2, 14)}[fmt]
    v = np.moveaxis(np.asarray(x, np.float32).astype(ml_dtypes.bfloat16).astype(np.float64), axis, -1)
    blocks = v.reshape(v.shape[:-1] + (-1, 32))
    amax = np.abs(blocks).max(-1, keepdims=True)
    byte = np.maximum(np.where(amax > 0, np.frexp(amax)[1] - 1 + 127, 0) - down, 1)
    scale = np.exp2(byte - 127.0)
    codes = (blocks / scale).astype(np.float32).astype(dtype).astype(np.float64)
    return np.moveaxis((codes * scale).reshape(v.shape), -1, axis)


WIDE = False


def mx_kscale(k):
    if not WIDE:
        return np.ones(k)
    levels = np.array([10, -10, 5, -5, 0])
    if k % 512:
        return np.exp2(np.random.permutation(np.resize(levels, k // 32))).repeat(32)
    a = np.empty((k // 512, 16))
    for p in range(k // 512):
        a[p, :8] = np.random.permutation(np.resize(levels, 8))
        for g in range(8):
            far = levels[np.abs(levels - a[p, g]) >= 10]
            a[p, g + 8] = far[np.random.randint(len(far))]
    return np.exp2(a.ravel()).repeat(32)


def f64(x):
    return np.asarray(x).astype(np.float64)


def striped(idx):
    return np.tile(idx.reshape(-1, 16).T, (8, 1)).astype(np.uint16)


def unstriped(offs):
    return offs[:16].T.reshape(-1).astype(np.int64)


def pack_weight(w):
    k, n = w.shape
    w = f64(np.asarray(w, np.float32).astype(ml_dtypes.bfloat16)).reshape(k // 32, 32, n)
    amax = np.abs(w).max(1)
    byte = np.clip(np.where(amax > 0, np.frexp(amax)[1] - 1 + 127 - 7, 1), 1, 254)
    scaled = (w * np.exp2(127.0 - byte)[:, None, :]).reshape(k, n).astype(np.float32)
    words = np.ascontiguousarray(scaled.reshape(k // 512, 128, 4, n).transpose(0, 1, 3, 2)).astype(ml_dtypes.float8_e4m3fn).view(np.uint8)
    return words, np.ascontiguousarray(byte.astype(np.uint8).reshape(k // 512, 16, n))


def unpack_weight(words, scales):
    g, p, n, _ = words.shape
    vals = np.ascontiguousarray(words).view(ml_dtypes.float8_e4m3fn).astype(np.float64) * np.repeat(np.exp2(scales.astype(np.float64) - 127.0), 8, axis=1)[..., None]
    return vals.transpose(0, 1, 3, 2).reshape(g * 512, n)


E2M1 = np.array([0.0, 0.5, 1.0, 1.5, 2.0, 3.0, 4.0, 6.0, -0.0, -0.5, -1.0, -1.5, -2.0, -3.0, -4.0, -6.0])


def pack_fp4(w):
    k, n = w.shape
    w = f64(np.asarray(w, np.float32).astype(ml_dtypes.bfloat16)).reshape(k // 32, 32, n)
    amax = np.abs(w).max(1)
    mant, ex = np.frexp(amax / 6.0)
    byte = np.clip(np.where(amax > 0, np.where(mant > 0.5, ex, ex - 1) + 127, 1), 1, 254)
    scaled = (w * np.exp2(127.0 - byte)[:, None, :]).reshape(k, n).astype(np.float32)
    c = np.ascontiguousarray(scaled.reshape(k // 512, 128, 4, n).transpose(0, 1, 3, 2)).astype(ml_dtypes.float4_e2m1fn).view(np.uint8) & 0xF
    words = (c[..., 0::2] | (c[..., 1::2] << 4)).reshape(k // 512, 128, 2 * n)
    return np.ascontiguousarray(words), np.ascontiguousarray(byte.astype(np.uint8).reshape(k // 512, 16, n))


def unpack_fp4(words, scales):
    g, _, n = scales.shape
    words = np.ascontiguousarray(words).reshape(g, 128, n, 2)
    nib = np.empty((g, 128, n, 4), np.uint8)
    nib[..., 0::2] = words & 0xF
    nib[..., 1::2] = words >> 4
    vals = E2M1[nib] * np.repeat(np.exp2(scales.astype(np.float64) - 127.0), 8, axis=1)[..., None]
    return vals.transpose(0, 1, 3, 2).reshape(g * 512, n)


def relu(v):
    return np.maximum(v, 0.0)


def sigmoid(v):
    return 1.0 / (1.0 + np.exp(-np.maximum(v, -700.0)))


K, T, S, N, H = 512, 1024, 512, 256, 512


def setup_inputs():
    n = np.random.standard_normal
    s = mx_kscale(K)[:, None]
    u = mx_kscale(H)
    packed_xT = pack_weight(n((K, T)) * s)
    packed_w1 = pack_fp4(n((K, H)) / np.sqrt(K) / s)
    packed_w2 = pack_fp4(n((K, H)) / np.sqrt(K) / s)
    packed_w3 = pack_fp4(n((H, N)) / np.sqrt(H) / u[:, None])
    return {
        "x_words": packed_xT[0],
        "x_scales": packed_xT[1],
        "w1_words": packed_w1[0],
        "w1_scales": packed_w1[1],
        "w2_words": packed_w2[0],
        "w2_scales": packed_w2[1],
        "slack": (np.random.uniform(0.2, 2.0, (H, S))).astype(np.float32),
        "unit": (np.random.uniform(0.6, 1.4, (H, 1)) * u[:, None]).astype(np.float32),
        "w3_words": packed_w3[0],
        "w3_scales": packed_w3[1],
        "offs": striped(np.random.permutation(T)[:S]),
        "pre": striped(np.random.permutation(S)),
        "suc": striped(np.random.permutation(S)),
        "req": striped(np.random.permutation(S)),
    }


def reference(x_words, x_scales, w1_words, w1_scales, w2_words, w2_scales, slack, unit, w3_words, w3_scales, offs, pre, suc, req):
    xq = unpack_weight(x_words, x_scales)[:, unstriped(offs)]
    px = unpack_fp4(w1_words, w1_scales).T @ xq
    dx1 = np.abs(px[:, unstriped(pre)] - px[:, unstriped(req)])
    py = unpack_fp4(w2_words, w2_scales).T @ xq
    dy1 = np.abs(py[:, unstriped(pre)] - py[:, unstriped(req)])
    dx2 = np.abs(px[:, unstriped(req)] - px[:, unstriped(suc)])
    dy2 = np.abs(py[:, unstriped(req)] - py[:, unstriped(suc)])
    dx3 = np.abs(px[:, unstriped(pre)] - px[:, unstriped(suc)])
    ins = dx1 + dy1 + dx2 + dy2 - dx3
    late = relu(0.5 * ins - f64(slack))
    hid = f64(unit) * (ins * (sigmoid(f64(slack) - late)))
    return unpack_fp4(w3_words, w3_scales).T @ mxq(hid, 0, "e4m3")

@@ -1,0 +1,234 @@
+from contextlib import ExitStack
+
+import concourse.mybir as mybir
+from concourse.masks import make_identity
+
+F32 = mybir.dt.float32
+BF16 = mybir.dt.bfloat16
+I32 = mybir.dt.int32
+U32 = mybir.dt.uint32
+U16 = mybir.dt.uint16
+U8 = mybir.dt.uint8
+FP8X4 = mybir.dt.float8_e4m3fn_x4
+FP4X4 = mybir.dt.float4_e2m1fn_x4
+ALU = mybir.AluOpType
+ACT = mybir.ActivationFunctionType
+
+K, T, S, N, H = 512, 1024, 512, 256, 512
+P = 128
+PACK = 4
+PART = 256
+
+FLOPS = 2 * K * H * S * 2 + 2 * H * N * S
+
+
+def load_scale_rows(queues, plane, rows):
+    for quad, queue in enumerate(queues):
+        queue.dma_start(out=plane[32 * quad : 32 * quad + 4, :].bitcast(I32), in_=rows[4 * quad : 4 * quad + 4, :].bitcast(I32))
+
+
+def tile_picked_ydarpi_soft_p_kernel(
+    tc, x_words, x_scales, w1_words, w1_scales, w2_words, w2_scales, slack, unit, w3_words, w3_scales, offs, pre, suc, req, out
+):
+    nc = tc.nc
+    with ExitStack() as ctx:
+        keep = ctx.enter_context(tc.tile_pool(name="keep", bufs=1))
+        work = ctx.enter_context(tc.tile_pool(name="work", bufs=8))
+        half = ctx.enter_context(tc.tile_pool(name="half", bufs=2))
+        ps_mm = ctx.enter_context(tc.psum_pool(name="ps_mm", bufs=2))
+        ps_diff = ctx.enter_context(tc.psum_pool(name="ps_diff", bufs=2))
+        ps_sum = ctx.enter_context(tc.psum_pool(name="ps_sum", bufs=3))
+        ps_out = ctx.enter_context(tc.psum_pool(name="ps_out", bufs=1))
+
+        offs_sb = keep.tile([P, S // 16], U16, name="offs_sb")
+        pre_sb = keep.tile([P, S // 16], U16, name="pre_sb")
+        suc_sb = keep.tile([P, S // 16], U16, name="suc_sb")
+        req_sb = keep.tile([P, S // 16], U16, name="req_sb")
+        x_tab = keep.tile([P, T], I32, name="x_tab", align_bytes=64)
+        x_sc_tab = keep.tile([P, T], U8, name="x_sc_tab", align_bytes=64)
+        w1_raw = keep.tile([P, 2 * H], U8, name="w1_raw", align_bytes=64)
+        w2_raw = keep.tile([P, 2 * H], U8, name="w2_raw", align_bytes=64)
+        w1_sc_raw = keep.tile([P, H], U8, name="w1_sc_raw", align_bytes=64)
+        w2_sc_raw = keep.tile([P, H], U8, name="w2_sc_raw", align_bytes=64)
+        w3_sb = keep.tile([P, 2 * N], U8, name="w3_sb", align_bytes=64)
+        slack_sb = keep.tile([P, PACK, S], F32, name="slack_sb")
+        unit_sb = keep.tile([P, PACK], F32, name="unit_sb")
+        ident = keep.tile([P, P], F32, name="ident", align_bytes=64)
+
+        nc.gpsimd.memset(x_sc_tab[:].bitcast(I32), 0)
+        nc.gpsimd.memset(w1_sc_raw[:].bitcast(I32), 0)
+        nc.gpsimd.memset(w2_sc_raw[:].bitcast(I32), 0)
+
+        nc.sync.dma_start(offs_sb[:], offs)
+        nc.scalar.dma_start(out=x_tab[:], in_=x_words[0].rearrange("p n t -> p (n t)").bitcast(I32))
+        load_scale_rows([nc.sync, nc.scalar, nc.sync, nc.scalar], x_sc_tab[:], x_scales[0])
+        nc.sync.dma_start(out=w1_raw[:].bitcast(I32), in_=w1_words[0].bitcast(I32))
+        load_scale_rows([nc.gpsimd, nc.gpsimd, nc.sync, nc.sync], w1_sc_raw[:], w1_scales[0])
+        nc.sync.dma_start(req_sb[:], req)
+        nc.sync.dma_start(out=w2_raw[:].bitcast(I32), in_=w2_words[0].bitcast(I32))
+        load_scale_rows([nc.sync] * 4, w2_sc_raw[:], w2_scales[0])
+        nc.sync.dma_start(pre_sb[:], pre)
+        nc.sync.dma_start(suc_sb[:], suc)
+        nc.sync.dma_start(out=slack_sb[:], in_=slack.rearrange("(p t) j -> p t j", t=PACK))
+        nc.sync.dma_start(out=unit_sb[:], in_=unit.rearrange("(p t) o -> p (t o)", t=PACK))
+        nc.sync.dma_start(out=w3_sb[:].bitcast(I32), in_=w3_words[0].bitcast(I32))
+        make_identity(nc, ident[:])
+
+        x_codes = keep.tile([P, S], U32, name="x_codes", align_bytes=64)
+        x_sc = keep.tile([P, S], U8, name="x_sc", align_bytes=64)
+        nc.vector.tensor_copy(out=x_sc[:], in_=x_sc_tab[:].indirect(offs_sb[:]))
+        nc.vector.tensor_copy(out=x_codes[:], in_=x_tab[:].bitcast(U32).indirect(offs_sb[:]))
+
+        dealt = []
+        for name, raw, sc_raw in (("w1", w1_raw, w1_sc_raw), ("w2", w2_raw, w2_sc_raw)):
+            words = keep.tile([P, 2 * H], U8, name=name + "_words", align_bytes=64)
+            sc = keep.tile([P, H], U8, name=name + "_sc", align_bytes=64)
+            nc.scalar.copy(
+                out=words[:].bitcast(U16).rearrange("p (t m) -> p t m", t=PACK),
+                in_=raw[:].bitcast(U16).rearrange("p (m t) -> p t m", t=PACK),
+            )
+            nc.gpsimd.tensor_copy(
+                out=sc[:].rearrange("p (t m) -> p t m", t=PACK),
+                in_=sc_raw[:].rearrange("p (m t) -> p t m", t=PACK),
+            )
+            dealt.append((words, sc))
+
+        w3_sc = w1_sc_raw[:, 0:N]
+        load_scale_rows([nc.sync] * 4, w3_sc, w3_scales[0])
+
+        px, py = {}, {}
+
+        units = [(j0, t) for j0 in range(0, S, PART) for t in range(PACK)]
+        planes = {}
+        for j0 in range(0, S, PART):
+            planes[j0] = half.tile([P, PACK, PART], BF16, name="planes", align_bytes=64)
+        tiles = {}
+
+        def fresh(name, k, width=PART, bufs=8):
+            made = work.tile([P, width], F32, name=name, bufs=bufs)
+            tiles.setdefault((name, k), made)
+            return made[:]
+
+        def got(name, k):
+            return tiles[(name, k)][:]
+
+        def project(name, t):
+            words, sc = dealt[0] if name == "px" else dealt[1]
+            acc = ps_mm.tile([P, S], F32, name="acc")
+            nc.tensor.matmul_mx(
+                out=acc[:],
+                lhsT=words[:, 2 * P * t : 2 * P * (t + 1)].bitcast(FP4X4),
+                lhsT_scale=sc[:, P * t : P * (t + 1)],
+                rhs=x_codes[:].bitcast(FP8X4),
+                rhs_scale=x_sc[:],
+                start=True,
+                stop=True,
+            )
+            row = keep.tile([P, S], F32, name="%s%d" % (name, t))
+            if (name, t) in ():
+                nc.vector.tensor_copy(out=row[:], in_=acc[:])
+            else:
+                nc.scalar.copy(out=row[:], in_=acc[:])
+            (px if name == "px" else py).setdefault(t, row)
+
+        def picked(rows, places, k):
+            j0, t = units[k]
+            return rows[t][:].indirect(places[:, j0 // 16 : (j0 + PART) // 16])
+
+        def x_request(k):
+            if k in range(8):
+                nc.vector.tensor_copy(out=fresh("x_req", k, bufs=8), in_=picked(px, req_sb, k))
+            else:
+                nc.scalar.activation(out=fresh("x_req", k, bufs=8), in_=picked(px, req_sb, k), func=ACT.Copy)
+
+        def x_leg(name, places, k):
+            nc.vector.tensor_tensor(out=fresh(name, k, bufs=2), in0=picked(px, places, k), in1=got("x_req", k), op=ALU.subtract)
+
+        def y_request(k):
+            nc.scalar.activation(out=fresh("y_neg", k, bufs=3), in_=picked(py, req_sb, k), func=ACT.Copy, scale=-1.0)
+
+        def add_turned(dst, first, second):
+            nc.tensor.matmul(out=dst, lhsT=first, rhs=ident[:], start=True, stop=False, is_transpose=True)
+            nc.tensor.matmul(out=dst, lhsT=second, rhs=ident[:], start=False, stop=True, is_transpose=True)
+
+        def y_leg(side, places, k):
+            stop_at = fresh("y_stop%d" % side, k, bufs=3)
+            nc.scalar.activation(out=stop_at, in_=picked(py, places, k), func=ACT.Copy)
+            if side == 0:
+                diff = ps_diff.tile([P, 2 * PART], F32, name="diff")
+                tiles.setdefault(("diff", k), diff)
+            for b in range(0, PART, P):
+                add_turned(got("diff", k)[:, side * PART + b : side * PART + b + P], stop_at[:, b : b + P], got("y_neg", k)[:, b : b + P])
+
+        def y_distance(k):
+            dist = fresh("dist", k, width=2 * PART, bufs=2)
+            nc.scalar.activation(out=dist, in_=got("diff", k), func=ACT.Abs)
+            y_sum = ps_sum.tile([P, PART], F32, name="y_sum")
+            tiles.setdefault(("y_sum", k), y_sum)
+            for b in range(0, PART, P):
+                add_turned(y_sum[:, b : b + P], dist[:, b : b + P], dist[:, PART + b : PART + b + P])
+
+        def fused(name, k, in0, scalar, in1, op0, op1):
+            nc.vector.scalar_tensor_tensor(out=fresh(name, k), in0=in0, scalar=scalar, in1=in1, op0=op0, op1=op1)
+
+        def slack_of(k):
+            j0, t = units[k]
+            return slack_sb[:, t, j0 : j0 + PART]
+
+        def hidden(k):
+            j0, t = units[k]
+            nc.vector.scalar_tensor_tensor(
+                out=planes[j0][:, t, :], in0=got("gate", k), scalar=unit_sb[:, t : t + 1], in1=got("ins", k), op0=ALU.mult, op1=ALU.mult
+            )
+
+        def finish(k):
+            j0, t = units[k]
+            if t != PACK - 1:
+                return
+            woven = half.tile([P, PART, PACK], BF16, name="woven", align_bytes=64)
+            if j0 in (0,):
+                nc.scalar.copy(out=woven[:], in_=planes[j0][:].rearrange("p t j -> p j t"))
+            else:
+                nc.vector.tensor_copy(out=woven[:], in_=planes[j0][:].rearrange("p t j -> p j t"))
+            codes = half.tile([P, PART], U32, name="codes", align_bytes=64)
+            scales = half.tile([P, PART], U8, name="scales", align_bytes=64)
+            nc.vector.quantize_mx(out=codes[:].bitcast(FP8X4), scales=scales[:], in_=woven[:].rearrange("p j t -> p (j t)"))
+            res = ps_out.tile([P, N // P, PART], F32, name="res")
+            for g in range(N // P):
+                nc.tensor.matmul_mx(
+                    out=res[:, g, :],
+                    lhsT=w3_sb[:, 2 * P * g : 2 * P * (g + 1)].bitcast(FP4X4),
+                    lhsT_scale=w3_sc[:, P * g : P * (g + 1)],
+                    rhs=codes[:].bitcast(FP8X4),
+                    rhs_scale=scales[:],
+                    start=True,
+                    stop=True,
+                )
+            res_sb = half.tile([P, N // P, PART], F32, name="res_sb")
+            nc.scalar.copy(out=res_sb[:], in_=res[:])
+            nc.sync.dma_start(out=out.rearrange("(g p) j -> p g j", p=P)[:, :, j0 : j0 + PART], in_=res_sb[:])
+
+        stages = [
+            (4, PACK, lambda k: project("px", k)),
+            (2, PACK, lambda k: project("py", k)),
+            (3, len(units), x_request),
+            (0, len(units), y_request),
+            (-1, len(units), y_distance),
+            (2, len(units), lambda k: x_leg("u", pre_sb, k)),
+            (-2, len(units), lambda k: fused("ins", k, got("e2", k), 2.0, got("y_sum", k), ALU.mult, ALU.add)),
+            (2, len(units), lambda k: x_leg("v", suc_sb, k)),
+            (-2, len(units), lambda k: fused("over", k, got("ins", k), 0.5, slack_of(k), ALU.mult, ALU.subtract)),
+            (2, len(units), lambda k: nc.vector.tensor_tensor(out=fresh("top", k), in0=got("u", k), in1=got("v", k), op=ALU.max)),
+            (-2, len(units), lambda k: fused("neg", k, got("over", k), 0.0, slack_of(k), ALU.max, ALU.subtract)),
+            (0, len(units), lambda k: y_leg(0, pre_sb, k)),
+            (-3, len(units), lambda k: nc.scalar.activation(out=fresh("gate", k), in_=got("neg", k), func=ACT.Sigmoid, scale=-1.0)),
+            (0, len(units), lambda k: y_leg(1, suc_sb, k)),
+            (2, len(units), lambda k: fused("e1", k, got("u", k), 0.0, got("top", k), ALU.max, ALU.subtract)),
+            (-4, len(units), hidden),
+            (2, len(units), lambda k: fused("e2", k, got("v", k), 0.0, got("e1", k), ALU.max, ALU.add)),
+            (-4, len(units), finish),
+        ]
+        for step in range(-5, len(units) + 6):
+            for lead, count, stage in stages:
+                if 0 <= step + lead < count:
+                    stage(step + lead)

@@ -33,12 +33,11 @@ def tile_picked_ydarpi_soft_p_kernel(
     nc = tc.nc
     with ExitStack() as ctx:
         keep = ctx.enter_context(tc.tile_pool(name="keep", bufs=1))
-        work = ctx.enter_context(tc.tile_pool(name="work", bufs=8))
+        work = ctx.enter_context(tc.tile_pool(name="work", bufs=4))
         half = ctx.enter_context(tc.tile_pool(name="half", bufs=2))
         ps_mm = ctx.enter_context(tc.psum_pool(name="ps_mm", bufs=2))
-        ps_diff = ctx.enter_context(tc.psum_pool(name="ps_diff", bufs=2))
+        ps_diff = ctx.enter_context(tc.psum_pool(name="ps_diff", bufs=3))
         ps_sum = ctx.enter_context(tc.psum_pool(name="ps_sum", bufs=3))
-        ps_out = ctx.enter_context(tc.psum_pool(name="ps_out", bufs=1))
 
         offs_sb = keep.tile([P, S // 16], U16, name="offs_sb")
         pre_sb = keep.tile([P, S // 16], U16, name="pre_sb")
@@ -51,36 +50,45 @@ def tile_picked_ydarpi_soft_p_kernel(
         w1_sc_raw = keep.tile([P, H], U8, name="w1_sc_raw", align_bytes=64)
         w2_sc_raw = keep.tile([P, H], U8, name="w2_sc_raw", align_bytes=64)
         w3_sb = keep.tile([P, 2 * N], U8, name="w3_sb", align_bytes=64)
-        slack_sb = keep.tile([P, PACK, S], F32, name="slack_sb")
         unit_sb = keep.tile([P, PACK], F32, name="unit_sb")
         ident = keep.tile([P, P], F32, name="ident", align_bytes=64)
 
-        nc.gpsimd.memset(x_sc_tab[:].bitcast(I32), 0)
-        nc.gpsimd.memset(w1_sc_raw[:].bitcast(I32), 0)
-        nc.gpsimd.memset(w2_sc_raw[:].bitcast(I32), 0)
+        nc.vector.memset(x_sc_tab[:].bitcast(I32), 0)
+        nc.vector.memset(w1_sc_raw[:].bitcast(I32), 0)
+        nc.vector.memset(w2_sc_raw[:].bitcast(I32), 0)
+        warm = keep.tile([P, 8], F32, name="warm")
+        nc.vector.memset(warm[:, 0:1], 0.0)
+        nc.scalar.activation(out=warm[:, 1:2], in_=warm[:, 0:1], func=ACT.Sigmoid)
 
         nc.sync.dma_start(offs_sb[:], offs)
-        nc.scalar.dma_start(out=x_tab[:], in_=x_words[0].rearrange("p n t -> p (n t)").bitcast(I32))
-        load_scale_rows([nc.sync, nc.scalar, nc.sync, nc.scalar], x_sc_tab[:], x_scales[0])
         nc.sync.dma_start(out=w1_raw[:].bitcast(I32), in_=w1_words[0].bitcast(I32))
-        load_scale_rows([nc.gpsimd, nc.gpsimd, nc.sync, nc.sync], w1_sc_raw[:], w1_scales[0])
         nc.sync.dma_start(req_sb[:], req)
-        nc.sync.dma_start(out=w2_raw[:].bitcast(I32), in_=w2_words[0].bitcast(I32))
-        load_scale_rows([nc.sync] * 4, w2_sc_raw[:], w2_scales[0])
+        load_scale_rows([nc.sync] * 4, x_sc_tab[:], x_scales[0])
+        nc.sync.dma_start(out=x_tab[:], in_=x_words[0].rearrange("p n t -> p (n t)").bitcast(I32))
+        load_scale_rows([nc.sync] * 4, w1_sc_raw[:], w1_scales[0])
+        nc.gpsimd.dma_start(out=w2_raw[:].bitcast(I32), in_=w2_words[0].bitcast(I32))
+        load_scale_rows([nc.sync] * 3 + [nc.gpsimd], w2_sc_raw[:], w2_scales[0])
         nc.sync.dma_start(pre_sb[:], pre)
         nc.sync.dma_start(suc_sb[:], suc)
-        nc.sync.dma_start(out=slack_sb[:], in_=slack.rearrange("(p t) j -> p t j", t=PACK))
+        make_identity(nc, ident[:])
+        slack_sb = {}
+        for j0 in range(0, S, PART):
+            slack_part = keep.tile([P, PACK, PART], F32, name="slack%d" % j0)
+            nc.sync.dma_start(out=slack_part[:], in_=slack.rearrange("(p t) j -> p t j", t=PACK)[:, :, j0 : j0 + PART])
+            slack_sb.setdefault(j0, slack_part)
         nc.sync.dma_start(out=unit_sb[:], in_=unit.rearrange("(p t) o -> p (t o)", t=PACK))
         nc.sync.dma_start(out=w3_sb[:].bitcast(I32), in_=w3_words[0].bitcast(I32))
-        make_identity(nc, ident[:])
 
         x_codes = keep.tile([P, S], U32, name="x_codes", align_bytes=64)
         x_sc = keep.tile([P, S], U8, name="x_sc", align_bytes=64)
         nc.vector.tensor_copy(out=x_sc[:], in_=x_sc_tab[:].indirect(offs_sb[:]))
-        nc.vector.tensor_copy(out=x_codes[:], in_=x_tab[:].bitcast(U32).indirect(offs_sb[:]))
+        for j0 in range(0, S, PART):
+            nc.vector.tensor_copy(
+                out=x_codes[:, j0 : j0 + PART], in_=x_tab[:].bitcast(U32).indirect(offs_sb[:, j0 // 16 : (j0 + PART) // 16])
+            )
 
-        dealt = []
-        for name, raw, sc_raw in (("w1", w1_raw, w1_sc_raw), ("w2", w2_raw, w2_sc_raw)):
+        dealt = {}
+        for name, raw, sc_raw in (("px", w1_raw, w1_sc_raw), ("py", w2_raw, w2_sc_raw)):
             words = keep.tile([P, 2 * H], U8, name=name + "_words", align_bytes=64)
             sc = keep.tile([P, H], U8, name=name + "_sc", align_bytes=64)
             nc.scalar.copy(
@@ -91,69 +99,78 @@ def tile_picked_ydarpi_soft_p_kernel(
                 out=sc[:].rearrange("p (t m) -> p t m", t=PACK),
                 in_=sc_raw[:].rearrange("p (m t) -> p t m", t=PACK),
             )
-            dealt.append((words, sc))
+            dealt.setdefault(name, (words, sc))
 
         w3_sc = w1_sc_raw[:, 0:N]
         load_scale_rows([nc.sync] * 4, w3_sc, w3_scales[0])
 
-        px, py = {}, {}
-
         units = [(j0, t) for j0 in range(0, S, PART) for t in range(PACK)]
+        groups = [(0, 1), (2, 3), (4, 5), (6,), (7,)]
+        group_of = {k: members for members in groups for k in members}
         planes = {}
         for j0 in range(0, S, PART):
-            planes[j0] = half.tile([P, PACK, PART], BF16, name="planes", align_bytes=64)
+            planes.setdefault(j0, half.tile([P, PACK, PART], BF16, name="planes", align_bytes=64))
         tiles = {}
 
-        def fresh(name, k, width=PART, bufs=8):
+        def fresh(name, key, width, bufs=4):
             made = work.tile([P, width], F32, name=name, bufs=bufs)
-            tiles.setdefault((name, k), made)
+            tiles.setdefault((name, key), made)
             return made[:]
 
-        def got(name, k):
-            return tiles[(name, k)][:]
+        def got(name, key):
+            return tiles[(name, key)][:]
+
+        def share(name, k):
+            at = PART * group_of[k].index(k)
+            return got(name, group_of[k])[:, at : at + PART]
 
         def project(name, t):
-            words, sc = dealt[0] if name == "px" else dealt[1]
+            words, sc = dealt[name]
             acc = ps_mm.tile([P, S], F32, name="acc")
-            nc.tensor.matmul_mx(
-                out=acc[:],
-                lhsT=words[:, 2 * P * t : 2 * P * (t + 1)].bitcast(FP4X4),
-                lhsT_scale=sc[:, P * t : P * (t + 1)],
-                rhs=x_codes[:].bitcast(FP8X4),
-                rhs_scale=x_sc[:],
-                start=True,
-                stop=True,
-            )
             row = keep.tile([P, S], F32, name="%s%d" % (name, t))
-            if (name, t) in ():
+            tiles.setdefault((name, t), row)
+            width = PART if (name, t) in (("px", 0),) else S
+            for j0 in range(0, S, width):
+                nc.tensor.matmul_mx(
+                    out=acc[:, j0 : j0 + width],
+                    lhsT=words[:, 2 * P * t : 2 * P * (t + 1)].bitcast(FP4X4),
+                    lhsT_scale=sc[:, P * t : P * (t + 1)],
+                    rhs=x_codes[:, j0 : j0 + width].bitcast(FP8X4),
+                    rhs_scale=x_sc[:, j0 : j0 + width],
+                    start=True,
+                    stop=True,
+                )
+            if (name, t) in [("px", t) for t in range(PACK)]:
                 nc.vector.tensor_copy(out=row[:], in_=acc[:])
             else:
                 nc.scalar.copy(out=row[:], in_=acc[:])
-            (px if name == "px" else py).setdefault(t, row)
 
-        def picked(rows, places, k):
+        def picked(name, places, k):
             j0, t = units[k]
-            return rows[t][:].indirect(places[:, j0 // 16 : (j0 + PART) // 16])
+            return got(name, t).indirect(places[:, j0 // 16 : (j0 + PART) // 16])
 
         def x_request(k):
-            if k in range(8):
-                nc.vector.tensor_copy(out=fresh("x_req", k, bufs=8), in_=picked(px, req_sb, k))
+            if k in range(PACK):
+                nc.vector.tensor_copy(out=fresh("x_req", k, PART, bufs=3), in_=picked("px", req_sb, k))
             else:
-                nc.scalar.activation(out=fresh("x_req", k, bufs=8), in_=picked(px, req_sb, k), func=ACT.Copy)
+                nc.scalar.activation(out=fresh("x_req", k, PART, bufs=3), in_=picked("px", req_sb, k), func=ACT.Copy)
 
         def x_leg(name, places, k):
-            nc.vector.tensor_tensor(out=fresh(name, k, bufs=2), in0=picked(px, places, k), in1=got("x_req", k), op=ALU.subtract)
+            members = group_of[k]
+            if k == members[0]:
+                fresh(name, members, PART * len(members), bufs=3)
+            nc.vector.tensor_tensor(out=share(name, k), in0=picked("px", places, k), in1=got("x_req", k), op=ALU.subtract)
 
         def y_request(k):
-            nc.scalar.activation(out=fresh("y_neg", k, bufs=3), in_=picked(py, req_sb, k), func=ACT.Copy, scale=-1.0)
+            nc.scalar.activation(out=fresh("y_neg", k, PART, bufs=2), in_=picked("py", req_sb, k), func=ACT.Copy, scale=-1.0)
 
         def add_turned(dst, first, second):
             nc.tensor.matmul(out=dst, lhsT=first, rhs=ident[:], start=True, stop=False, is_transpose=True)
             nc.tensor.matmul(out=dst, lhsT=second, rhs=ident[:], start=False, stop=True, is_transpose=True)
 
         def y_leg(side, places, k):
-            stop_at = fresh("y_stop%d" % side, k, bufs=3)
-            nc.scalar.activation(out=stop_at, in_=picked(py, places, k), func=ACT.Copy)
+            stop_at = fresh("y_stop%d" % side, k, PART, bufs=2)
+            nc.scalar.activation(out=stop_at, in_=picked("py", places, k), func=ACT.Copy)
             if side == 0:
                 diff = ps_diff.tile([P, 2 * PART], F32, name="diff")
                 tiles.setdefault(("diff", k), diff)
@@ -161,74 +178,98 @@ def tile_picked_ydarpi_soft_p_kernel(
                 add_turned(got("diff", k)[:, side * PART + b : side * PART + b + P], stop_at[:, b : b + P], got("y_neg", k)[:, b : b + P])
 
         def y_distance(k):
-            dist = fresh("dist", k, width=2 * PART, bufs=2)
+            members = group_of[k]
+            dist = fresh("dist", k, 2 * PART, bufs=2)
             nc.scalar.activation(out=dist, in_=got("diff", k), func=ACT.Abs)
-            y_sum = ps_sum.tile([P, PART], F32, name="y_sum")
-            tiles.setdefault(("y_sum", k), y_sum)
+            if k == members[0]:
+                y_sum = ps_sum.tile([P, PART * len(members)], F32, name="y_sum")
+                tiles.setdefault(("y_sum", members), y_sum)
             for b in range(0, PART, P):
-                add_turned(y_sum[:, b : b + P], dist[:, b : b + P], dist[:, PART + b : PART + b + P])
+                add_turned(share("y_sum", k)[:, b : b + P], dist[:, b : b + P], dist[:, PART + b : PART + b + P])
 
-        def fused(name, k, in0, scalar, in1, op0, op1):
-            nc.vector.scalar_tensor_tensor(out=fresh(name, k), in0=in0, scalar=scalar, in1=in1, op0=op0, op1=op1)
+        def slack_of(members):
+            j0, t = units[members[0]]
+            return slack_sb[j0][:].rearrange("p t j -> p (t j)")[:, PART * t : PART * (t + len(members))]
 
-        def slack_of(k):
-            j0, t = units[k]
-            return slack_sb[:, t, j0 : j0 + PART]
+        def whole_group(stage):
+            def run(k):
+                members = group_of[k]
+                if k == members[-1]:
+                    stage(members, PART * len(members))
+
+            return run
+
+        def fused(name, in0, scalar, in1, op0, op1):
+            def stage(members, width):
+                second = slack_of(members) if in1 == "slack" else got(in1, members)
+                nc.vector.scalar_tensor_tensor(out=fresh(name, members, width), in0=got(in0, members), scalar=scalar, in1=second, op0=op0, op1=op1)
+
+            return whole_group(stage)
+
+        def larger(members, width):
+            nc.vector.tensor_tensor(out=fresh("top", members, width), in0=got("u", members), in1=got("v", members), op=ALU.max)
+
+        def gate(members, width):
+            nc.scalar.activation(out=fresh("gate", members, width), in_=got("neg", members), func=ACT.Sigmoid, scale=-1.0)
 
         def hidden(k):
             j0, t = units[k]
             nc.vector.scalar_tensor_tensor(
-                out=planes[j0][:, t, :], in0=got("gate", k), scalar=unit_sb[:, t : t + 1], in1=got("ins", k), op0=ALU.mult, op1=ALU.mult
+                out=planes[j0][:, t, :], in0=share("gate", k), scalar=unit_sb[:, t : t + 1], in1=share("ins", k), op0=ALU.mult, op1=ALU.mult
             )
 
         def finish(k):
             j0, t = units[k]
             if t != PACK - 1:
                 return
-            woven = half.tile([P, PART, PACK], BF16, name="woven", align_bytes=64)
-            if j0 in (0,):
-                nc.scalar.copy(out=woven[:], in_=planes[j0][:].rearrange("p t j -> p j t"))
-            else:
-                nc.vector.tensor_copy(out=woven[:], in_=planes[j0][:].rearrange("p t j -> p j t"))
-            codes = half.tile([P, PART], U32, name="codes", align_bytes=64)
-            scales = half.tile([P, PART], U8, name="scales", align_bytes=64)
-            nc.vector.quantize_mx(out=codes[:].bitcast(FP8X4), scales=scales[:], in_=woven[:].rearrange("p j t -> p (j t)"))
-            res = ps_out.tile([P, N // P, PART], F32, name="res")
-            for g in range(N // P):
-                nc.tensor.matmul_mx(
-                    out=res[:, g, :],
-                    lhsT=w3_sb[:, 2 * P * g : 2 * P * (g + 1)].bitcast(FP4X4),
-                    lhsT_scale=w3_sc[:, P * g : P * (g + 1)],
-                    rhs=codes[:].bitcast(FP8X4),
-                    rhs_scale=scales[:],
-                    start=True,
-                    stop=True,
-                )
-            res_sb = half.tile([P, N // P, PART], F32, name="res_sb")
-            nc.scalar.copy(out=res_sb[:], in_=res[:])
-            nc.sync.dma_start(out=out.rearrange("(g p) j -> p g j", p=P)[:, :, j0 : j0 + PART], in_=res_sb[:])
+            last = k == len(units) - 1
+            width = P if last else PART
+            for c0 in range(0, PART, width):
+                woven = half.tile([P, width, PACK], BF16, name="woven", align_bytes=64)
+                if j0 in (0,):
+                    nc.scalar.copy(out=woven[:], in_=planes[j0][:, :, c0 : c0 + width].rearrange("p t j -> p j t"))
+                else:
+                    nc.vector.tensor_copy(out=woven[:], in_=planes[j0][:, :, c0 : c0 + width].rearrange("p t j -> p j t"))
+                codes = half.tile([P, width], U32, name="codes", align_bytes=64)
+                scales = half.tile([P, width], U8, name="scales", align_bytes=64)
+                nc.vector.quantize_mx(out=codes[:].bitcast(FP8X4), scales=scales[:], in_=woven[:].rearrange("p j t -> p (j t)"))
+                res = ps_mm.tile([P, N // P, width], F32, name="acc")
+                for g in range(N // P):
+                    nc.tensor.matmul_mx(
+                        out=res[:, g, :],
+                        lhsT=w3_sb[:, 2 * P * g : 2 * P * (g + 1)].bitcast(FP4X4),
+                        lhsT_scale=w3_sc[:, P * g : P * (g + 1)],
+                        rhs=codes[:].bitcast(FP8X4),
+                        rhs_scale=scales[:],
+                        start=True,
+                        stop=True,
+                    )
+                res_sb = half.tile([P, N // P, width], F32, name="res_sb", bufs=3)
+                nc.scalar.copy(out=res_sb[:], in_=res[:])
+                nc.sync.dma_start(out=out.rearrange("(g p) j -> p g j", p=P)[:, :, j0 + c0 : j0 + c0 + width], in_=res_sb[:])
 
+        count = len(units)
         stages = [
-            (4, PACK, lambda k: project("px", k)),
-            (2, PACK, lambda k: project("py", k)),
-            (3, len(units), x_request),
-            (0, len(units), y_request),
-            (-1, len(units), y_distance),
-            (2, len(units), lambda k: x_leg("u", pre_sb, k)),
-            (-2, len(units), lambda k: fused("ins", k, got("e2", k), 2.0, got("y_sum", k), ALU.mult, ALU.add)),
-            (2, len(units), lambda k: x_leg("v", suc_sb, k)),
-            (-2, len(units), lambda k: fused("over", k, got("ins", k), 0.5, slack_of(k), ALU.mult, ALU.subtract)),
-            (2, len(units), lambda k: nc.vector.tensor_tensor(out=fresh("top", k), in0=got("u", k), in1=got("v", k), op=ALU.max)),
-            (-2, len(units), lambda k: fused("neg", k, got("over", k), 0.0, slack_of(k), ALU.max, ALU.subtract)),
-            (0, len(units), lambda k: y_leg(0, pre_sb, k)),
-            (-3, len(units), lambda k: nc.scalar.activation(out=fresh("gate", k), in_=got("neg", k), func=ACT.Sigmoid, scale=-1.0)),
-            (0, len(units), lambda k: y_leg(1, suc_sb, k)),
-            (2, len(units), lambda k: fused("e1", k, got("u", k), 0.0, got("top", k), ALU.max, ALU.subtract)),
-            (-4, len(units), hidden),
-            (2, len(units), lambda k: fused("e2", k, got("v", k), 0.0, got("e1", k), ALU.max, ALU.add)),
-            (-4, len(units), finish),
+            (3, PACK, lambda k: project("px", k)),
+            (3, PACK, lambda k: project("py", k)),
+            (2, count, x_request),
+            (1, count, y_request),
+            (-1, count, y_distance),
+            (1, count, lambda k: x_leg("u", pre_sb, k)),
+            (-2, count, fused("ins", "e2", 2.0, "y_sum", ALU.mult, ALU.add)),
+            (1, count, lambda k: x_leg("v", suc_sb, k)),
+            (-2, count, fused("over", "ins", 0.5, "slack", ALU.mult, ALU.subtract)),
+            (1, count, whole_group(larger)),
+            (-2, count, fused("neg", "over", 0.0, "slack", ALU.max, ALU.subtract)),
+            (1, count, lambda k: y_leg(0, pre_sb, k)),
+            (-3, count, whole_group(gate)),
+            (1, count, lambda k: y_leg(1, suc_sb, k)),
+            (1, count, fused("e1", "u", 0.0, "top", ALU.max, ALU.subtract)),
+            (-5, count, hidden),
+            (1, count, fused("e2", "v", 0.0, "e1", ALU.max, ALU.add)),
+            (-5, count, finish),
         ]
-        for step in range(-5, len(units) + 6):
-            for lead, count, stage in stages:
-                if 0 <= step + lead < count:
+        for step in range(-5, count + 8):
+            for lead, limit, stage in stages:
+                if 0 <= step + lead < limit:
                     stage(step + lead)

@@ -106,6 +106,7 @@ def tile_picked_ydarpi_soft_p_kernel(
 
         units = [(j0, t) for j0 in range(0, S, PART) for t in range(PACK)]
         groups = [(0, 1), (2, 3), (4, 5), (6,), (7,)]
+        by_median = groups[3:]
         group_of = {k: members for members in groups for k in members}
         planes = {}
         for j0 in range(0, S, PART):
@@ -199,15 +200,38 @@ def tile_picked_ydarpi_soft_p_kernel(
 
             return run
 
-        def fused(name, in0, scalar, in1, op0, op1):
-            def stage(members, width):
-                second = slack_of(members) if in1 == "slack" else got(in1, members)
-                nc.vector.scalar_tensor_tensor(out=fresh(name, members, width), in0=got(in0, members), scalar=scalar, in1=second, op0=op0, op1=op1)
+        def fused(name, members, in0, scalar, in1, op0, op1):
+            made = fresh(name, members, PART * len(members))
+            nc.vector.scalar_tensor_tensor(out=made, in0=got(in0, members), scalar=scalar, in1=in1, op0=op0, op1=op1)
 
-            return whole_group(stage)
+        def x_first(members, width):
+            if members in by_median:
+                fused("top", members, "u", 0.0, got("v", members), ALU.max, ALU.min)
+            else:
+                nc.vector.tensor_tensor(out=fresh("top", members, width), in0=got("u", members), in1=got("v", members), op=ALU.max)
 
-        def larger(members, width):
-            nc.vector.tensor_tensor(out=fresh("top", members, width), in0=got("u", members), in1=got("v", members), op=ALU.max)
+        def x_second(members, width):
+            if members in by_median:
+                fused("e1", members, "u", 0.0, got("top", members), ALU.min, ALU.max)
+            else:
+                fused("e1", members, "u", 0.0, got("top", members), ALU.max, ALU.subtract)
+
+        def x_third(members, width):
+            if members not in by_median:
+                fused("e2", members, "v", 0.0, got("e1", members), ALU.max, ALU.add)
+
+        def x_distance(members, width):
+            if members in by_median:
+                nc.scalar.activation(out=fresh("e2", members, width), in_=got("e1", members), func=ACT.Abs)
+
+        def detour(members, width):
+            fused("ins", members, "e2", 2.0, got("y_sum", members), ALU.mult, ALU.add)
+
+        def over(members, width):
+            fused("over", members, "ins", 0.5, slack_of(members), ALU.mult, ALU.subtract)
+
+        def late(members, width):
+            fused("neg", members, "over", 0.0, slack_of(members), ALU.max, ALU.subtract)
 
         def gate(members, width):
             nc.scalar.activation(out=fresh("gate", members, width), in_=got("neg", members), func=ACT.Sigmoid, scale=-1.0)
@@ -227,9 +251,9 @@ def tile_picked_ydarpi_soft_p_kernel(
             for c0 in range(0, PART, width):
                 woven = half.tile([P, width, PACK], BF16, name="woven", align_bytes=64)
                 if j0 in (0,):
-                    nc.scalar.copy(out=woven[:], in_=planes[j0][:, :, c0 : c0 + width].rearrange("p t j -> p j t"))
+                    nc.scalar.copy(out=woven[:].rearrange("p (c i) t -> p c t i", i=4), in_=planes[j0][:, :, c0 : c0 + width].rearrange("p t (c i) -> p c t i", i=4))
                 else:
-                    nc.vector.tensor_copy(out=woven[:], in_=planes[j0][:, :, c0 : c0 + width].rearrange("p t j -> p j t"))
+                    nc.vector.tensor_copy(out=woven[:].rearrange("p (c i) t -> p c t i", i=4), in_=planes[j0][:, :, c0 : c0 + width].rearrange("p t (c i) -> p c t i", i=4))
                 codes = half.tile([P, width], U32, name="codes", align_bytes=64)
                 scales = half.tile([P, width], U8, name="scales", align_bytes=64)
                 nc.vector.quantize_mx(out=codes[:].bitcast(FP8X4), scales=scales[:], in_=woven[:].rearrange("p j t -> p (j t)"))
@@ -255,18 +279,19 @@ def tile_picked_ydarpi_soft_p_kernel(
             (2, count, x_request),
             (1, count, y_request),
             (-1, count, y_distance),
+            (-1, count, whole_group(x_distance)),
             (1, count, lambda k: x_leg("u", pre_sb, k)),
-            (-2, count, fused("ins", "e2", 2.0, "y_sum", ALU.mult, ALU.add)),
+            (-2, count, whole_group(detour)),
             (1, count, lambda k: x_leg("v", suc_sb, k)),
-            (-2, count, fused("over", "ins", 0.5, "slack", ALU.mult, ALU.subtract)),
-            (1, count, whole_group(larger)),
-            (-2, count, fused("neg", "over", 0.0, "slack", ALU.max, ALU.subtract)),
+            (-2, count, whole_group(over)),
+            (1, count, whole_group(x_first)),
+            (-2, count, whole_group(late)),
             (1, count, lambda k: y_leg(0, pre_sb, k)),
             (-3, count, whole_group(gate)),
             (1, count, lambda k: y_leg(1, suc_sb, k)),
-            (1, count, fused("e1", "u", 0.0, "top", ALU.max, ALU.subtract)),
+            (1, count, whole_group(x_second)),
             (-5, count, hidden),
-            (1, count, fused("e2", "v", 0.0, "e1", ALU.max, ALU.add)),
+            (1, count, whole_group(x_third)),
             (-5, count, finish),
         ]
         for step in range(-5, count + 8):

@@ -17,7 +17,16 @@ ACT = mybir.ActivationFunctionType
 K, T, S, N, H = 512, 1024, 512, 256, 512
 P = 128
 PACK = 4
-PART = 256
+HALF = S // 2
+LIST_COLUMN = 16
+RUN = 4
+
+PRODUCT_LEAD = 2
+DISTANCE_LAG = 2
+HIDDEN_LAG = 6
+X_BUFFERS = 3
+Y_BUFFERS = 2
+WORK_BUFFERS = 4
 
 FLOPS = 2 * K * H * S * 2 + 2 * H * N * S
 
@@ -33,29 +42,30 @@ def tile_picked_ydarpi_soft_p_kernel(
     nc = tc.nc
     with ExitStack() as ctx:
         keep = ctx.enter_context(tc.tile_pool(name="keep", bufs=1))
-        work = ctx.enter_context(tc.tile_pool(name="work", bufs=4))
-        half = ctx.enter_context(tc.tile_pool(name="half", bufs=2))
-        ps_mm = ctx.enter_context(tc.psum_pool(name="ps_mm", bufs=2))
+        work = ctx.enter_context(tc.tile_pool(name="work", bufs=WORK_BUFFERS))
+        per_half = ctx.enter_context(tc.tile_pool(name="per_half", bufs=2))
+        ps_mx = ctx.enter_context(tc.psum_pool(name="ps_mx", bufs=2))
         ps_diff = ctx.enter_context(tc.psum_pool(name="ps_diff", bufs=3))
         ps_sum = ctx.enter_context(tc.psum_pool(name="ps_sum", bufs=3))
 
-        offs_sb = keep.tile([P, S // 16], U16, name="offs_sb")
-        pre_sb = keep.tile([P, S // 16], U16, name="pre_sb")
-        suc_sb = keep.tile([P, S // 16], U16, name="suc_sb")
-        req_sb = keep.tile([P, S // 16], U16, name="req_sb")
-        x_tab = keep.tile([P, T], I32, name="x_tab", align_bytes=64)
-        x_sc_tab = keep.tile([P, T], U8, name="x_sc_tab", align_bytes=64)
+        offs_sb = keep.tile([P, S // LIST_COLUMN], U16, name="offs_sb")
+        pre_sb = keep.tile([P, S // LIST_COLUMN], U16, name="pre_sb")
+        suc_sb = keep.tile([P, S // LIST_COLUMN], U16, name="suc_sb")
+        req_sb = keep.tile([P, S // LIST_COLUMN], U16, name="req_sb")
+        x_table = keep.tile([P, T], I32, name="x_table", align_bytes=64)
+        x_scale_table = keep.tile([P, T], U8, name="x_scale_table", align_bytes=64)
         w1_raw = keep.tile([P, 2 * H], U8, name="w1_raw", align_bytes=64)
         w2_raw = keep.tile([P, 2 * H], U8, name="w2_raw", align_bytes=64)
-        w1_sc_raw = keep.tile([P, H], U8, name="w1_sc_raw", align_bytes=64)
-        w2_sc_raw = keep.tile([P, H], U8, name="w2_sc_raw", align_bytes=64)
+        w1_scale_raw = keep.tile([P, H], U8, name="w1_scale_raw", align_bytes=64)
+        w2_scale_raw = keep.tile([P, H], U8, name="w2_scale_raw", align_bytes=64)
         w3_sb = keep.tile([P, 2 * N], U8, name="w3_sb", align_bytes=64)
         unit_sb = keep.tile([P, PACK], F32, name="unit_sb")
         ident = keep.tile([P, P], F32, name="ident", align_bytes=64)
 
-        nc.vector.memset(x_sc_tab[:].bitcast(I32), 0)
-        nc.vector.memset(w1_sc_raw[:].bitcast(I32), 0)
-        nc.vector.memset(w2_sc_raw[:].bitcast(I32), 0)
+        nc.vector.memset(x_scale_table[:].bitcast(I32), 0)
+        nc.vector.memset(w1_scale_raw[:].bitcast(I32), 0)
+        nc.vector.memset(w2_scale_raw[:].bitcast(I32), 0)
+
         warm = keep.tile([P, 8], F32, name="warm")
         nc.vector.memset(warm[:, 0:1], 0.0)
         nc.scalar.activation(out=warm[:, 1:2], in_=warm[:, 0:1], func=ACT.Sigmoid)
@@ -63,238 +73,245 @@ def tile_picked_ydarpi_soft_p_kernel(
         nc.sync.dma_start(offs_sb[:], offs)
         nc.sync.dma_start(out=w1_raw[:].bitcast(I32), in_=w1_words[0].bitcast(I32))
         nc.sync.dma_start(req_sb[:], req)
-        load_scale_rows([nc.sync] * 4, x_sc_tab[:], x_scales[0])
-        nc.sync.dma_start(out=x_tab[:], in_=x_words[0].rearrange("p n t -> p (n t)").bitcast(I32))
-        load_scale_rows([nc.sync] * 4, w1_sc_raw[:], w1_scales[0])
+        load_scale_rows([nc.sync] * 4, x_scale_table[:], x_scales[0])
+        nc.sync.dma_start(out=x_table[:], in_=x_words[0].rearrange("p n t -> p (n t)").bitcast(I32))
+        load_scale_rows([nc.sync] * 4, w1_scale_raw[:], w1_scales[0])
         nc.gpsimd.dma_start(out=w2_raw[:].bitcast(I32), in_=w2_words[0].bitcast(I32))
-        load_scale_rows([nc.sync] * 3 + [nc.gpsimd], w2_sc_raw[:], w2_scales[0])
+        load_scale_rows([nc.sync] * 3 + [nc.gpsimd], w2_scale_raw[:], w2_scales[0])
         nc.sync.dma_start(pre_sb[:], pre)
         nc.sync.dma_start(suc_sb[:], suc)
         make_identity(nc, ident[:])
+
         slack_sb = {}
-        for j0 in range(0, S, PART):
-            slack_part = keep.tile([P, PACK, PART], F32, name="slack%d" % j0)
-            nc.sync.dma_start(out=slack_part[:], in_=slack.rearrange("(p t) j -> p t j", t=PACK)[:, :, j0 : j0 + PART])
-            slack_sb.setdefault(j0, slack_part)
+        for j0 in range(0, S, HALF):
+            slack_half = keep.tile([P, PACK, HALF], F32, name="slack%d" % j0)
+            nc.sync.dma_start(out=slack_half[:], in_=slack.rearrange("(p t) j -> p t j", t=PACK)[:, :, j0 : j0 + HALF])
+            slack_sb.setdefault(j0, slack_half)
         nc.sync.dma_start(out=unit_sb[:], in_=unit.rearrange("(p t) o -> p (t o)", t=PACK))
         nc.sync.dma_start(out=w3_sb[:].bitcast(I32), in_=w3_words[0].bitcast(I32))
 
-        x_codes = keep.tile([P, S], U32, name="x_codes", align_bytes=64)
-        x_sc = keep.tile([P, S], U8, name="x_sc", align_bytes=64)
-        nc.vector.tensor_copy(out=x_sc[:], in_=x_sc_tab[:].indirect(offs_sb[:]))
-        for j0 in range(0, S, PART):
-            nc.vector.tensor_copy(
-                out=x_codes[:, j0 : j0 + PART], in_=x_tab[:].bitcast(U32).indirect(offs_sb[:, j0 // 16 : (j0 + PART) // 16])
-            )
+        def entries(places, j0):
+            return places[:, j0 // LIST_COLUMN : (j0 + HALF) // LIST_COLUMN]
+
+        x_scale = keep.tile([P, S], U8, name="x_scale", align_bytes=64)
+        nc.vector.tensor_copy(out=x_scale[:], in_=x_scale_table[:].indirect(offs_sb[:]))
+        x_codes = {}
+        for j0 in range(0, S, HALF):
+            picked_words = keep.tile([P, HALF], U32, name="x_codes%d" % j0, align_bytes=64)
+            nc.vector.tensor_copy(out=picked_words[:], in_=x_table[:].bitcast(U32).indirect(entries(offs_sb, j0)))
+            x_codes.setdefault(j0, picked_words)
 
         dealt = {}
-        for name, raw, sc_raw in (("px", w1_raw, w1_sc_raw), ("py", w2_raw, w2_sc_raw)):
-            words = keep.tile([P, 2 * H], U8, name=name + "_words", align_bytes=64)
-            sc = keep.tile([P, H], U8, name=name + "_sc", align_bytes=64)
+        for axis, raw, scale_raw in (("px", w1_raw, w1_scale_raw), ("py", w2_raw, w2_scale_raw)):
+            w_words = keep.tile([P, 2 * H], U8, name=axis + "_words", align_bytes=64)
+            w_scale = keep.tile([P, H], U8, name=axis + "_scale", align_bytes=64)
             nc.scalar.copy(
-                out=words[:].bitcast(U16).rearrange("p (t m) -> p t m", t=PACK),
+                out=w_words[:].bitcast(U16).rearrange("p (t m) -> p t m", t=PACK),
                 in_=raw[:].bitcast(U16).rearrange("p (m t) -> p t m", t=PACK),
             )
-            nc.gpsimd.tensor_copy(
-                out=sc[:].rearrange("p (t m) -> p t m", t=PACK),
-                in_=sc_raw[:].rearrange("p (m t) -> p t m", t=PACK),
-            )
-            dealt.setdefault(name, (words, sc))
+            for t0, t1 in ((0, 1), (1, PACK)):
+                nc.gpsimd.tensor_copy(
+                    out=w_scale[:].rearrange("p (t m) -> p t m", t=PACK)[:, t0:t1, :],
+                    in_=scale_raw[:].rearrange("p (m t) -> p t m", t=PACK)[:, t0:t1, :],
+                )
+            dealt.setdefault(axis, (w_words, w_scale))
 
-        w3_sc = w1_sc_raw[:, 0:N]
-        load_scale_rows([nc.sync] * 4, w3_sc, w3_scales[0])
+        w3_scale = w1_scale_raw[:, 0:N]
+        load_scale_rows([nc.sync] * 4, w3_scale, w3_scales[0])
 
-        units = [(j0, t) for j0 in range(0, S, PART) for t in range(PACK)]
-        groups = [(0, 1), (2, 3), (4, 5), (6,), (7,)]
-        by_median = groups[3:]
-        group_of = {k: members for members in groups for k in members}
-        planes = {}
-        for j0 in range(0, S, PART):
-            planes.setdefault(j0, half.tile([P, PACK, PART], BF16, name="planes", align_bytes=64))
+        units = [(j0, t) for j0 in range(0, S, HALF) for t in range(PACK)]
+        count = len(units)
+        pairs = [(k, k + 1) for k in range(0, count - 2, 2)]
+        singles = [(k,) for k in range(count - 2, count)]
+        group_of = {k: group for group in pairs + singles for k in group}
+        hid_rows = {}
+        for j0 in range(0, S, HALF):
+            hid_rows.setdefault(j0, per_half.tile([P, PACK, HALF], BF16, name="hid_rows", align_bytes=64))
         tiles = {}
 
-        def fresh(name, key, width, bufs=4):
+        def fresh(name, key, width, bufs=WORK_BUFFERS):
             made = work.tile([P, width], F32, name=name, bufs=bufs)
             tiles.setdefault((name, key), made)
             return made[:]
+
+        def fresh_for(name, group, bufs=WORK_BUFFERS):
+            return fresh(name, group, HALF * len(group), bufs)
 
         def got(name, key):
             return tiles[(name, key)][:]
 
         def share(name, k):
-            at = PART * group_of[k].index(k)
-            return got(name, group_of[k])[:, at : at + PART]
+            at = HALF * group_of[k].index(k)
+            return got(name, group_of[k])[:, at : at + HALF]
 
-        def project(name, t):
-            words, sc = dealt[name]
-            acc = ps_mm.tile([P, S], F32, name="acc")
-            row = keep.tile([P, S], F32, name="%s%d" % (name, t))
-            tiles.setdefault((name, t), row)
-            width = PART if (name, t) in (("px", 0),) else S
-            for j0 in range(0, S, width):
+        def product(axis, t):
+            w_words, w_scale = dealt[axis]
+            acc = ps_mx.tile([P, S], F32, name="acc")
+            row = keep.tile([P, S], F32, name="%s%d" % (axis, t))
+            tiles.setdefault((axis, t), row)
+            for j0 in range(0, S, HALF):
                 nc.tensor.matmul_mx(
-                    out=acc[:, j0 : j0 + width],
-                    lhsT=words[:, 2 * P * t : 2 * P * (t + 1)].bitcast(FP4X4),
-                    lhsT_scale=sc[:, P * t : P * (t + 1)],
-                    rhs=x_codes[:, j0 : j0 + width].bitcast(FP8X4),
-                    rhs_scale=x_sc[:, j0 : j0 + width],
+                    out=acc[:, j0 : j0 + HALF],
+                    lhsT=w_words[:, 2 * P * t : 2 * P * (t + 1)].bitcast(FP4X4),
+                    lhsT_scale=w_scale[:, P * t : P * (t + 1)],
+                    rhs=x_codes[j0][:].bitcast(FP8X4),
+                    rhs_scale=x_scale[:, j0 : j0 + HALF],
                     start=True,
                     stop=True,
                 )
-            if (name, t) in [("px", t) for t in range(PACK)]:
+            if axis == "px":
                 nc.vector.tensor_copy(out=row[:], in_=acc[:])
             else:
                 nc.scalar.copy(out=row[:], in_=acc[:])
 
-        def picked(name, places, k):
+        def picked(axis, places, k):
             j0, t = units[k]
-            return got(name, t).indirect(places[:, j0 // 16 : (j0 + PART) // 16])
+            return got(axis, t).indirect(entries(places, j0))
 
         def x_request(k):
-            if k in range(PACK):
-                nc.vector.tensor_copy(out=fresh("x_req", k, PART, bufs=3), in_=picked("px", req_sb, k))
+            x_req = fresh("x_req", k, HALF, X_BUFFERS)
+            if k < PACK:
+                nc.vector.tensor_copy(out=x_req, in_=picked("px", req_sb, k))
             else:
-                nc.scalar.activation(out=fresh("x_req", k, PART, bufs=3), in_=picked("px", req_sb, k), func=ACT.Copy)
+                nc.scalar.activation(out=x_req, in_=picked("px", req_sb, k), func=ACT.Copy)
 
         def x_leg(name, places, k):
-            members = group_of[k]
-            if k == members[0]:
-                fresh(name, members, PART * len(members), bufs=3)
+            if k == group_of[k][0]:
+                fresh_for(name, group_of[k], X_BUFFERS)
             nc.vector.tensor_tensor(out=share(name, k), in0=picked("px", places, k), in1=got("x_req", k), op=ALU.subtract)
 
         def y_request(k):
-            nc.scalar.activation(out=fresh("y_neg", k, PART, bufs=2), in_=picked("py", req_sb, k), func=ACT.Copy, scale=-1.0)
+            nc.scalar.activation(out=fresh("y_req_neg", k, HALF, Y_BUFFERS), in_=picked("py", req_sb, k), func=ACT.Copy, scale=-1.0)
 
         def add_turned(dst, first, second):
             nc.tensor.matmul(out=dst, lhsT=first, rhs=ident[:], start=True, stop=False, is_transpose=True)
             nc.tensor.matmul(out=dst, lhsT=second, rhs=ident[:], start=False, stop=True, is_transpose=True)
 
         def y_leg(side, places, k):
-            stop_at = fresh("y_stop%d" % side, k, PART, bufs=2)
-            nc.scalar.activation(out=stop_at, in_=picked("py", places, k), func=ACT.Copy)
+            y_stop = fresh("y_stop%d" % side, k, HALF, Y_BUFFERS)
+            nc.scalar.activation(out=y_stop, in_=picked("py", places, k), func=ACT.Copy)
             if side == 0:
-                diff = ps_diff.tile([P, 2 * PART], F32, name="diff")
-                tiles.setdefault(("diff", k), diff)
-            for b in range(0, PART, P):
-                add_turned(got("diff", k)[:, side * PART + b : side * PART + b + P], stop_at[:, b : b + P], got("y_neg", k)[:, b : b + P])
+                y_diff = ps_diff.tile([P, 2 * HALF], F32, name="y_diff")
+                tiles.setdefault(("y_diff", k), y_diff)
+            for b in range(0, HALF, P):
+                at = side * HALF + b
+                add_turned(got("y_diff", k)[:, at : at + P], y_stop[:, b : b + P], got("y_req_neg", k)[:, b : b + P])
 
         def y_distance(k):
-            members = group_of[k]
-            dist = fresh("dist", k, 2 * PART, bufs=2)
-            nc.scalar.activation(out=dist, in_=got("diff", k), func=ACT.Abs)
-            if k == members[0]:
-                y_sum = ps_sum.tile([P, PART * len(members)], F32, name="y_sum")
-                tiles.setdefault(("y_sum", members), y_sum)
-            for b in range(0, PART, P):
-                add_turned(share("y_sum", k)[:, b : b + P], dist[:, b : b + P], dist[:, PART + b : PART + b + P])
+            y_dist = fresh("y_dist", k, 2 * HALF, Y_BUFFERS)
+            nc.scalar.activation(out=y_dist, in_=got("y_diff", k), func=ACT.Abs)
+            if k == group_of[k][0]:
+                y_sum = ps_sum.tile([P, HALF * len(group_of[k])], F32, name="y_sum")
+                tiles.setdefault(("y_sum", group_of[k]), y_sum)
+            for b in range(0, HALF, P):
+                add_turned(share("y_sum", k)[:, b : b + P], y_dist[:, b : b + P], y_dist[:, HALF + b : HALF + b + P])
 
-        def slack_of(members):
-            j0, t = units[members[0]]
-            return slack_sb[j0][:].rearrange("p t j -> p (t j)")[:, PART * t : PART * (t + len(members))]
+        def slack_of(group):
+            j0, t = units[group[0]]
+            return slack_sb[j0][:].rearrange("p t j -> p (t j)")[:, HALF * t : HALF * (t + len(group))]
 
         def whole_group(stage):
             def run(k):
-                members = group_of[k]
-                if k == members[-1]:
-                    stage(members, PART * len(members))
+                if k == group_of[k][-1]:
+                    stage(group_of[k])
 
             return run
 
-        def fused(name, members, in0, scalar, in1, op0, op1):
-            made = fresh(name, members, PART * len(members))
-            nc.vector.scalar_tensor_tensor(out=made, in0=got(in0, members), scalar=scalar, in1=in1, op0=op0, op1=op1)
+        def fused(name, group, in0, scalar, in1, op0, op1):
+            nc.vector.scalar_tensor_tensor(out=fresh_for(name, group), in0=got(in0, group), scalar=scalar, in1=in1, op0=op0, op1=op1)
 
-        def x_first(members, width):
-            if members in by_median:
-                fused("top", members, "u", 0.0, got("v", members), ALU.max, ALU.min)
+        def x_step1(group):
+            if group in singles:
+                fused("x_step1", group, "u", 0.0, got("v", group), ALU.max, ALU.min)
             else:
-                nc.vector.tensor_tensor(out=fresh("top", members, width), in0=got("u", members), in1=got("v", members), op=ALU.max)
+                nc.vector.tensor_tensor(out=fresh_for("x_step1", group), in0=got("u", group), in1=got("v", group), op=ALU.max)
 
-        def x_second(members, width):
-            if members in by_median:
-                fused("e1", members, "u", 0.0, got("top", members), ALU.min, ALU.max)
+        def x_step2(group):
+            if group in singles:
+                fused("x_step2", group, "u", 0.0, got("x_step1", group), ALU.min, ALU.max)
             else:
-                fused("e1", members, "u", 0.0, got("top", members), ALU.max, ALU.subtract)
+                fused("x_step2", group, "u", 0.0, got("x_step1", group), ALU.max, ALU.subtract)
 
-        def x_third(members, width):
-            if members not in by_median:
-                fused("e2", members, "v", 0.0, got("e1", members), ALU.max, ALU.add)
+        def x_half_of_pair(group):
+            if group in pairs:
+                fused("x_half", group, "v", 0.0, got("x_step2", group), ALU.max, ALU.add)
 
-        def x_distance(members, width):
-            if members in by_median:
-                nc.scalar.activation(out=fresh("e2", members, width), in_=got("e1", members), func=ACT.Abs)
+        def x_half_of_single(group):
+            if group in singles:
+                nc.scalar.activation(out=fresh_for("x_half", group), in_=got("x_step2", group), func=ACT.Abs)
 
-        def detour(members, width):
-            fused("ins", members, "e2", 2.0, got("y_sum", members), ALU.mult, ALU.add)
+        def detour(group):
+            fused("ins", group, "x_half", 2.0, got("y_sum", group), ALU.mult, ALU.add)
 
-        def over(members, width):
-            fused("over", members, "ins", 0.5, slack_of(members), ALU.mult, ALU.subtract)
+        def over_slack(group):
+            fused("over", group, "ins", 0.5, slack_of(group), ALU.mult, ALU.subtract)
 
-        def late(members, width):
-            fused("neg", members, "over", 0.0, slack_of(members), ALU.max, ALU.subtract)
+        def late_less_slack(group):
+            fused("late_less_slack", group, "over", 0.0, slack_of(group), ALU.max, ALU.subtract)
 
-        def gate(members, width):
-            nc.scalar.activation(out=fresh("gate", members, width), in_=got("neg", members), func=ACT.Sigmoid, scale=-1.0)
+        def gate(group):
+            nc.scalar.activation(out=fresh_for("gate", group), in_=got("late_less_slack", group), func=ACT.Sigmoid, scale=-1.0)
 
         def hidden(k):
             j0, t = units[k]
             nc.vector.scalar_tensor_tensor(
-                out=planes[j0][:, t, :], in0=share("gate", k), scalar=unit_sb[:, t : t + 1], in1=share("ins", k), op0=ALU.mult, op1=ALU.mult
+                out=hid_rows[j0][:, t, :], in0=share("gate", k), scalar=unit_sb[:, t : t + 1], in1=share("ins", k), op0=ALU.mult, op1=ALU.mult
             )
 
-        def finish(k):
+        def last_product(k):
             j0, t = units[k]
             if t != PACK - 1:
                 return
-            last = k == len(units) - 1
-            width = P if last else PART
-            for c0 in range(0, PART, width):
-                woven = half.tile([P, width, PACK], BF16, name="woven", align_bytes=64)
-                if j0 in (0,):
-                    nc.scalar.copy(out=woven[:].rearrange("p (c i) t -> p c t i", i=4), in_=planes[j0][:, :, c0 : c0 + width].rearrange("p t (c i) -> p c t i", i=4))
+            last = k == count - 1
+            width = P if last else HALF
+            for c0 in range(0, HALF, width):
+                woven = per_half.tile([P, width, PACK], BF16, name="woven", align_bytes=64)
+                target = woven[:].rearrange("p (c i) t -> p c t i", i=RUN)
+                source = hid_rows[j0][:, :, c0 : c0 + width].rearrange("p t (c i) -> p c t i", i=RUN)
+                if last:
+                    nc.vector.tensor_copy(out=target, in_=source)
                 else:
-                    nc.vector.tensor_copy(out=woven[:].rearrange("p (c i) t -> p c t i", i=4), in_=planes[j0][:, :, c0 : c0 + width].rearrange("p t (c i) -> p c t i", i=4))
-                codes = half.tile([P, width], U32, name="codes", align_bytes=64)
-                scales = half.tile([P, width], U8, name="scales", align_bytes=64)
-                nc.vector.quantize_mx(out=codes[:].bitcast(FP8X4), scales=scales[:], in_=woven[:].rearrange("p j t -> p (j t)"))
-                res = ps_mm.tile([P, N // P, width], F32, name="acc")
+                    nc.scalar.copy(out=target, in_=source)
+                hid_codes = per_half.tile([P, width], U32, name="hid_codes", align_bytes=64)
+                hid_scale = per_half.tile([P, width], U8, name="hid_scale", align_bytes=64)
+                nc.vector.quantize_mx(out=hid_codes[:].bitcast(FP8X4), scales=hid_scale[:], in_=woven[:].rearrange("p j t -> p (j t)"))
+                acc = ps_mx.tile([P, N // P, width], F32, name="acc")
                 for g in range(N // P):
                     nc.tensor.matmul_mx(
-                        out=res[:, g, :],
+                        out=acc[:, g, :],
                         lhsT=w3_sb[:, 2 * P * g : 2 * P * (g + 1)].bitcast(FP4X4),
-                        lhsT_scale=w3_sc[:, P * g : P * (g + 1)],
-                        rhs=codes[:].bitcast(FP8X4),
-                        rhs_scale=scales[:],
+                        lhsT_scale=w3_scale[:, P * g : P * (g + 1)],
+                        rhs=hid_codes[:].bitcast(FP8X4),
+                        rhs_scale=hid_scale[:],
                         start=True,
                         stop=True,
                     )
-                res_sb = half.tile([P, N // P, width], F32, name="res_sb", bufs=3)
-                nc.scalar.copy(out=res_sb[:], in_=res[:])
-                nc.sync.dma_start(out=out.rearrange("(g p) j -> p g j", p=P)[:, :, j0 + c0 : j0 + c0 + width], in_=res_sb[:])
+                result = per_half.tile([P, N // P, width], F32, name="result", bufs=3)
+                nc.scalar.copy(out=result[:], in_=acc[:])
+                nc.sync.dma_start(out=out.rearrange("(g p) j -> p g j", p=P)[:, :, j0 + c0 : j0 + c0 + width], in_=result[:])
 
-        count = len(units)
         stages = [
-            (3, PACK, lambda k: project("px", k)),
-            (3, PACK, lambda k: project("py", k)),
-            (2, count, x_request),
-            (1, count, y_request),
-            (-1, count, y_distance),
-            (-1, count, whole_group(x_distance)),
-            (1, count, lambda k: x_leg("u", pre_sb, k)),
-            (-2, count, whole_group(detour)),
-            (1, count, lambda k: x_leg("v", suc_sb, k)),
-            (-2, count, whole_group(over)),
-            (1, count, whole_group(x_first)),
-            (-2, count, whole_group(late)),
-            (1, count, lambda k: y_leg(0, pre_sb, k)),
-            (-3, count, whole_group(gate)),
-            (1, count, lambda k: y_leg(1, suc_sb, k)),
-            (1, count, whole_group(x_second)),
-            (-5, count, hidden),
-            (1, count, whole_group(x_third)),
-            (-5, count, finish),
+            (PRODUCT_LEAD, PACK, lambda t: product("px", t)),
+            (PRODUCT_LEAD, PACK, lambda t: product("py", t)),
+            (1, count, x_request),
+            (0, count, y_request),
+            (-DISTANCE_LAG, count, y_distance),
+            (-DISTANCE_LAG, count, whole_group(x_half_of_single)),
+            (0, count, lambda k: x_leg("u", pre_sb, k)),
+            (-DISTANCE_LAG - 1, count, whole_group(detour)),
+            (0, count, lambda k: x_leg("v", suc_sb, k)),
+            (-DISTANCE_LAG - 1, count, whole_group(over_slack)),
+            (0, count, whole_group(x_step1)),
+            (-DISTANCE_LAG - 1, count, whole_group(late_less_slack)),
+            (0, count, lambda k: y_leg(0, pre_sb, k)),
+            (-DISTANCE_LAG - 2, count, whole_group(gate)),
+            (0, count, lambda k: y_leg(1, suc_sb, k)),
+            (0, count, whole_group(x_step2)),
+            (-HIDDEN_LAG, count, hidden),
+            (0, count, whole_group(x_half_of_pair)),
+            (-HIDDEN_LAG, count, last_product),
         ]
-        for step in range(-5, count + 8):
-            for lead, limit, stage in stages:
-                if 0 <= step + lead < limit:
-                    stage(step + lead)
+        for step in range(-PRODUCT_LEAD, count + HIDDEN_LAG):
+            for ahead, limit, stage in stages:
+                if 0 <= step + ahead < limit:
+                    stage(step + ahead)

from contextlib import ExitStack

import concourse.mybir as mybir
from concourse.masks import make_identity

F32 = mybir.dt.float32
BF16 = mybir.dt.bfloat16
I32 = mybir.dt.int32
U32 = mybir.dt.uint32
U16 = mybir.dt.uint16
U8 = mybir.dt.uint8
FP8X4 = mybir.dt.float8_e4m3fn_x4
FP4X4 = mybir.dt.float4_e2m1fn_x4
ALU = mybir.AluOpType
ACT = mybir.ActivationFunctionType

K, T, S, N, H = 512, 1024, 512, 256, 512
P = 128
PACK = 4
HALF = S // 2
LIST_COLUMN = 16
RUN = 4

PRODUCT_LEAD = 2
DISTANCE_LAG = 2
HIDDEN_LAG = 6
X_BUFFERS = 3
Y_BUFFERS = 2
WORK_BUFFERS = 4

FLOPS = 2 * K * H * S * 2 + 2 * H * N * S


def load_scale_rows(queues, plane, rows):
    for quad, queue in enumerate(queues):
        queue.dma_start(out=plane[32 * quad : 32 * quad + 4, :].bitcast(I32), in_=rows[4 * quad : 4 * quad + 4, :].bitcast(I32))


def tile_picked_ydarpi_soft_p_kernel(
    tc, x_words, x_scales, w1_words, w1_scales, w2_words, w2_scales, slack, unit, w3_words, w3_scales, offs, pre, suc, req, out
):
    nc = tc.nc
    with ExitStack() as ctx:
        keep = ctx.enter_context(tc.tile_pool(name="keep", bufs=1))
        work = ctx.enter_context(tc.tile_pool(name="work", bufs=WORK_BUFFERS))
        per_half = ctx.enter_context(tc.tile_pool(name="per_half", bufs=2))
        ps_mx = ctx.enter_context(tc.psum_pool(name="ps_mx", bufs=2))
        ps_diff = ctx.enter_context(tc.psum_pool(name="ps_diff", bufs=3))
        ps_sum = ctx.enter_context(tc.psum_pool(name="ps_sum", bufs=3))

        offs_sb = keep.tile([P, S // LIST_COLUMN], U16, name="offs_sb")
        pre_sb = keep.tile([P, S // LIST_COLUMN], U16, name="pre_sb")
        suc_sb = keep.tile([P, S // LIST_COLUMN], U16, name="suc_sb")
        req_sb = keep.tile([P, S // LIST_COLUMN], U16, name="req_sb")
        x_table = keep.tile([P, T], I32, name="x_table", align_bytes=64)
        x_scale_table = keep.tile([P, T], U8, name="x_scale_table", align_bytes=64)
        w1_raw = keep.tile([P, 2 * H], U8, name="w1_raw", align_bytes=64)
        w2_raw = keep.tile([P, 2 * H], U8, name="w2_raw", align_bytes=64)
        w1_scale_raw = keep.tile([P, H], U8, name="w1_scale_raw", align_bytes=64)
        w2_scale_raw = keep.tile([P, H], U8, name="w2_scale_raw", align_bytes=64)
        w3_sb = keep.tile([P, 2 * N], U8, name="w3_sb", align_bytes=64)
        unit_sb = keep.tile([P, PACK], F32, name="unit_sb")
        ident = keep.tile([P, P], F32, name="ident", align_bytes=64)

        nc.vector.memset(x_scale_table[:].bitcast(I32), 0)
        nc.vector.memset(w1_scale_raw[:].bitcast(I32), 0)
        nc.vector.memset(w2_scale_raw[:].bitcast(I32), 0)

        warm = keep.tile([P, 8], F32, name="warm")
        nc.vector.memset(warm[:, 0:1], 0.0)
        nc.scalar.activation(out=warm[:, 1:2], in_=warm[:, 0:1], func=ACT.Sigmoid)

        nc.sync.dma_start(offs_sb[:], offs)
        nc.sync.dma_start(out=w1_raw[:].bitcast(I32), in_=w1_words[0].bitcast(I32))
        nc.sync.dma_start(req_sb[:], req)
        load_scale_rows([nc.sync] * 4, x_scale_table[:], x_scales[0])
        nc.sync.dma_start(out=x_table[:], in_=x_words[0].rearrange("p n t -> p (n t)").bitcast(I32))
        load_scale_rows([nc.sync] * 4, w1_scale_raw[:], w1_scales[0])
        nc.gpsimd.dma_start(out=w2_raw[:].bitcast(I32), in_=w2_words[0].bitcast(I32))
        load_scale_rows([nc.sync] * 3 + [nc.gpsimd], w2_scale_raw[:], w2_scales[0])
        nc.sync.dma_start(pre_sb[:], pre)
        nc.sync.dma_start(suc_sb[:], suc)
        make_identity(nc, ident[:])

        slack_sb = {}
        for j0 in range(0, S, HALF):
            slack_half = keep.tile([P, PACK, HALF], F32, name="slack%d" % j0)
            nc.sync.dma_start(out=slack_half[:], in_=slack.rearrange("(p t) j -> p t j", t=PACK)[:, :, j0 : j0 + HALF])
            slack_sb.setdefault(j0, slack_half)
        nc.sync.dma_start(out=unit_sb[:], in_=unit.rearrange("(p t) o -> p (t o)", t=PACK))
        nc.sync.dma_start(out=w3_sb[:].bitcast(I32), in_=w3_words[0].bitcast(I32))

        def entries(places, j0):
            return places[:, j0 // LIST_COLUMN : (j0 + HALF) // LIST_COLUMN]

        x_scale = keep.tile([P, S], U8, name="x_scale", align_bytes=64)
        nc.vector.tensor_copy(out=x_scale[:], in_=x_scale_table[:].indirect(offs_sb[:]))
        x_codes = {}
        for j0 in range(0, S, HALF):
            picked_words = keep.tile([P, HALF], U32, name="x_codes%d" % j0, align_bytes=64)
            nc.vector.tensor_copy(out=picked_words[:], in_=x_table[:].bitcast(U32).indirect(entries(offs_sb, j0)))
            x_codes.setdefault(j0, picked_words)

        dealt = {}
        for axis, raw, scale_raw in (("px", w1_raw, w1_scale_raw), ("py", w2_raw, w2_scale_raw)):
            w_words = keep.tile([P, 2 * H], U8, name=axis + "_words", align_bytes=64)
            w_scale = keep.tile([P, H], U8, name=axis + "_scale", align_bytes=64)
            nc.scalar.copy(
                out=w_words[:].bitcast(U16).rearrange("p (t m) -> p t m", t=PACK),
                in_=raw[:].bitcast(U16).rearrange("p (m t) -> p t m", t=PACK),
            )
            for t0, t1 in ((0, 1), (1, PACK)):
                nc.gpsimd.tensor_copy(
                    out=w_scale[:].rearrange("p (t m) -> p t m", t=PACK)[:, t0:t1, :],
                    in_=scale_raw[:].rearrange("p (m t) -> p t m", t=PACK)[:, t0:t1, :],
                )
            dealt.setdefault(axis, (w_words, w_scale))

        w3_scale = w1_scale_raw[:, 0:N]
        load_scale_rows([nc.sync] * 4, w3_scale, w3_scales[0])

        units = [(j0, t) for j0 in range(0, S, HALF) for t in range(PACK)]
        count = len(units)
        pairs = [(k, k + 1) for k in range(0, count - 2, 2)]
        singles = [(k,) for k in range(count - 2, count)]
        group_of = {k: group for group in pairs + singles for k in group}
        hid_rows = {}
        for j0 in range(0, S, HALF):
            hid_rows.setdefault(j0, per_half.tile([P, PACK, HALF], BF16, name="hid_rows", align_bytes=64))
        tiles = {}

        def fresh(name, key, width, bufs=WORK_BUFFERS):
            made = work.tile([P, width], F32, name=name, bufs=bufs)
            tiles.setdefault((name, key), made)
            return made[:]

        def fresh_for(name, group, bufs=WORK_BUFFERS):
            return fresh(name, group, HALF * len(group), bufs)

        def got(name, key):
            return tiles[(name, key)][:]

        def share(name, k):
            at = HALF * group_of[k].index(k)
            return got(name, group_of[k])[:, at : at + HALF]

        def product(axis, t):
            w_words, w_scale = dealt[axis]
            acc = ps_mx.tile([P, S], F32, name="acc")
            row = keep.tile([P, S], F32, name="%s%d" % (axis, t))
            tiles.setdefault((axis, t), row)
            for j0 in range(0, S, HALF):
                nc.tensor.matmul_mx(
                    out=acc[:, j0 : j0 + HALF],
                    lhsT=w_words[:, 2 * P * t : 2 * P * (t + 1)].bitcast(FP4X4),
                    lhsT_scale=w_scale[:, P * t : P * (t + 1)],
                    rhs=x_codes[j0][:].bitcast(FP8X4),
                    rhs_scale=x_scale[:, j0 : j0 + HALF],
                    start=True,
                    stop=True,
                )
            if axis == "px":
                nc.vector.tensor_copy(out=row[:], in_=acc[:])
            else:
                nc.scalar.copy(out=row[:], in_=acc[:])

        def picked(axis, places, k):
            j0, t = units[k]
            return got(axis, t).indirect(entries(places, j0))

        def x_request(k):
            x_req = fresh("x_req", k, HALF, X_BUFFERS)
            if k < PACK:
                nc.vector.tensor_copy(out=x_req, in_=picked("px", req_sb, k))
            else:
                nc.scalar.activation(out=x_req, in_=picked("px", req_sb, k), func=ACT.Copy)

        def x_leg(name, places, k):
            if k == group_of[k][0]:
                fresh_for(name, group_of[k], X_BUFFERS)
            nc.vector.tensor_tensor(out=share(name, k), in0=picked("px", places, k), in1=got("x_req", k), op=ALU.subtract)

        def y_request(k):
            nc.scalar.activation(out=fresh("y_req_neg", k, HALF, Y_BUFFERS), in_=picked("py", req_sb, k), func=ACT.Copy, scale=-1.0)

        def add_turned(dst, first, second):
            nc.tensor.matmul(out=dst, lhsT=first, rhs=ident[:], start=True, stop=False, is_transpose=True)
            nc.tensor.matmul(out=dst, lhsT=second, rhs=ident[:], start=False, stop=True, is_transpose=True)

        def y_leg(side, places, k):
            y_stop = fresh("y_stop%d" % side, k, HALF, Y_BUFFERS)
            nc.scalar.activation(out=y_stop, in_=picked("py", places, k), func=ACT.Copy)
            if side == 0:
                y_diff = ps_diff.tile([P, 2 * HALF], F32, name="y_diff")
                tiles.setdefault(("y_diff", k), y_diff)
            for b in range(0, HALF, P):
                at = side * HALF + b
                add_turned(got("y_diff", k)[:, at : at + P], y_stop[:, b : b + P], got("y_req_neg", k)[:, b : b + P])

        def y_distance(k):
            y_dist = fresh("y_dist", k, 2 * HALF, Y_BUFFERS)
            nc.scalar.activation(out=y_dist, in_=got("y_diff", k), func=ACT.Abs)
            if k == group_of[k][0]:
                y_sum = ps_sum.tile([P, HALF * len(group_of[k])], F32, name="y_sum")
                tiles.setdefault(("y_sum", group_of[k]), y_sum)
            for b in range(0, HALF, P):
                add_turned(share("y_sum", k)[:, b : b + P], y_dist[:, b : b + P], y_dist[:, HALF + b : HALF + b + P])

        def slack_of(group):
            j0, t = units[group[0]]
            return slack_sb[j0][:].rearrange("p t j -> p (t j)")[:, HALF * t : HALF * (t + len(group))]

        def whole_group(stage):
            def run(k):
                if k == group_of[k][-1]:
                    stage(group_of[k])

            return run

        def fused(name, group, in0, scalar, in1, op0, op1):
            nc.vector.scalar_tensor_tensor(out=fresh_for(name, group), in0=got(in0, group), scalar=scalar, in1=in1, op0=op0, op1=op1)

        def x_step1(group):
            if group in singles:
                fused("x_step1", group, "u", 0.0, got("v", group), ALU.max, ALU.min)
            else:
                nc.vector.tensor_tensor(out=fresh_for("x_step1", group), in0=got("u", group), in1=got("v", group), op=ALU.max)

        def x_step2(group):
            if group in singles:
                fused("x_step2", group, "u", 0.0, got("x_step1", group), ALU.min, ALU.max)
            else:
                fused("x_step2", group, "u", 0.0, got("x_step1", group), ALU.max, ALU.subtract)

        def x_half_of_pair(group):
            if group in pairs:
                fused("x_half", group, "v", 0.0, got("x_step2", group), ALU.max, ALU.add)

        def x_half_of_single(group):
            if group in singles:
                nc.scalar.activation(out=fresh_for("x_half", group), in_=got("x_step2", group), func=ACT.Abs)

        def detour(group):
            fused("ins", group, "x_half", 2.0, got("y_sum", group), ALU.mult, ALU.add)

        def over_slack(group):
            fused("over", group, "ins", 0.5, slack_of(group), ALU.mult, ALU.subtract)

        def late_less_slack(group):
            fused("late_less_slack", group, "over", 0.0, slack_of(group), ALU.max, ALU.subtract)

        def gate(group):
            nc.scalar.activation(out=fresh_for("gate", group), in_=got("late_less_slack", group), func=ACT.Sigmoid, scale=-1.0)

        def hidden(k):
            j0, t = units[k]
            nc.vector.scalar_tensor_tensor(
                out=hid_rows[j0][:, t, :], in0=share("gate", k), scalar=unit_sb[:, t : t + 1], in1=share("ins", k), op0=ALU.mult, op1=ALU.mult
            )

        def last_product(k):
            j0, t = units[k]
            if t != PACK - 1:
                return
            last = k == count - 1
            width = P if last else HALF
            for c0 in range(0, HALF, width):
                woven = per_half.tile([P, width, PACK], BF16, name="woven", align_bytes=64)
                target = woven[:].rearrange("p (c i) t -> p c t i", i=RUN)
                source = hid_rows[j0][:, :, c0 : c0 + width].rearrange("p t (c i) -> p c t i", i=RUN)
                if last:
                    nc.vector.tensor_copy(out=target, in_=source)
                else:
                    nc.scalar.copy(out=target, in_=source)
                hid_codes = per_half.tile([P, width], U32, name="hid_codes", align_bytes=64)
                hid_scale = per_half.tile([P, width], U8, name="hid_scale", align_bytes=64)
                nc.vector.quantize_mx(out=hid_codes[:].bitcast(FP8X4), scales=hid_scale[:], in_=woven[:].rearrange("p j t -> p (j t)"))
                acc = ps_mx.tile([P, N // P, width], F32, name="acc")
                for g in range(N // P):
                    nc.tensor.matmul_mx(
                        out=acc[:, g, :],
                        lhsT=w3_sb[:, 2 * P * g : 2 * P * (g + 1)].bitcast(FP4X4),
                        lhsT_scale=w3_scale[:, P * g : P * (g + 1)],
                        rhs=hid_codes[:].bitcast(FP8X4),
                        rhs_scale=hid_scale[:],
                        start=True,
                        stop=True,
                    )
                result = per_half.tile([P, N // P, width], F32, name="result", bufs=3)
                nc.scalar.copy(out=result[:], in_=acc[:])
                nc.sync.dma_start(out=out.rearrange("(g p) j -> p g j", p=P)[:, :, j0 + c0 : j0 + c0 + width], in_=result[:])

        stages = [
            (PRODUCT_LEAD, PACK, lambda t: product("px", t)),
            (PRODUCT_LEAD, PACK, lambda t: product("py", t)),
            (1, count, x_request),
            (0, count, y_request),
            (-DISTANCE_LAG, count, y_distance),
            (-DISTANCE_LAG, count, whole_group(x_half_of_single)),
            (0, count, lambda k: x_leg("u", pre_sb, k)),
            (-DISTANCE_LAG - 1, count, whole_group(detour)),
            (0, count, lambda k: x_leg("v", suc_sb, k)),
            (-DISTANCE_LAG - 1, count, whole_group(over_slack)),
            (0, count, whole_group(x_step1)),
            (-DISTANCE_LAG - 1, count, whole_group(late_less_slack)),
            (0, count, lambda k: y_leg(0, pre_sb, k)),
            (-DISTANCE_LAG - 2, count, whole_group(gate)),
            (0, count, lambda k: y_leg(1, suc_sb, k)),
            (0, count, whole_group(x_step2)),
            (-HIDDEN_LAG, count, hidden),
            (0, count, whole_group(x_half_of_pair)),
            (-HIDDEN_LAG, count, last_product),
        ]
        for step in range(-PRODUCT_LEAD, count + HIDDEN_LAG):
            for ahead, limit, stage in stages:
                if 0 <= step + ahead < limit:
                    stage(step + ahead)
